import numpy as np
import ml_dtypes


def mxq(x, axis, fmt="e4m3"):
    dtype, down = {"e4m3": (ml_dtypes.float8_e4m3fn, 7), "e5m2": (ml_dtypes.float8_e5m2, 14)}[fmt]
    v = np.moveaxis(np.asarray(x, np.float32).astype(ml_dtypes.bfloat16).astype(np.float64), axis, -1)
    blocks = v.reshape(v.shape[:-1] + (-1, 32))
    amax = np.abs(blocks).max(-1, keepdims=True)
    byte = np.maximum(np.where(amax > 0, np.frexp(amax)[1] - 1 + 127, 0) - down, 1)
    scale = np.exp2(byte - 127.0)
    codes = (blocks / scale).astype(np.float32).astype(dtype).astype(np.float64)
    return np.moveaxis((codes * scale).reshape(v.shape), -1, axis)


WIDE = False


def mx_kscale(k):
    if not WIDE:
        return np.ones(k)
    levels = np.array([10, -10, 5, -5, 0])
    if k % 512:
        return np.exp2(np.random.permutation(np.resize(levels, k // 32))).repeat(32)
    a = np.empty((k // 512, 16))
    for p in range(k // 512):
        a[p, :8] = np.random.permutation(np.resize(levels, 8))
        for g in range(8):
            far = levels[np.abs(levels - a[p, g]) >= 10]
            a[p, g + 8] = far[np.random.randint(len(far))]
    return np.exp2(a.ravel()).repeat(32)


def f64(x):
    return np.asarray(x).astype(np.float64)


def striped8(idx):
    return np.asarray(idx).reshape(8, -1, 16).transpose(0, 2, 1).reshape(128, -1).astype(np.uint16)


def unstriped8(offs):
    return offs.reshape(8, 16, -1).transpose(0, 2, 1).reshape(8, -1).astype(np.int64)


def pick8(x, idx, run):
    r = np.arange(len(x))
    return x[r[:, None], idx[r % (8 * run) // run]]


E2M1 = np.array([0.0, 0.5, 1.0, 1.5, 2.0, 3.0, 4.0, 6.0, -0.0, -0.5, -1.0, -1.5, -2.0, -3.0, -4.0, -6.0])


def pack_weight(w, fmt):
    k, n = w.shape
    w = f64(np.asarray(w, np.float32).astype(ml_dtypes.bfloat16)).reshape(k // 32, 32, n)
    amax = np.abs(w).max(1)
    if fmt == "e4m3":
        byte = np.frexp(amax)[1] - 1 + 127 - 7
    else:
        mant, ex = np.frexp(amax / 6.0)
        byte = np.where(mant > 0.5, ex, ex - 1) + 127
    byte = np.clip(np.where(amax > 0, byte, 1), 1, 254)
    scaled = (w * np.exp2(127.0 - byte)[:, None, :]).reshape(k, n).astype(np.float32)
    by_word = np.ascontiguousarray(scaled.reshape(k // 512, 128, 4, n).transpose(0, 1, 3, 2))
    if fmt == "e4m3":
        words = by_word.astype(ml_dtypes.float8_e4m3fn).view(np.uint8)
    else:
        c = by_word.astype(ml_dtypes.float4_e2m1fn).view(np.uint8) & 0xF
        words = (c[..., 0::2] | (c[..., 1::2] << 4)).reshape(k // 512, 128, 2 * n)
    return np.ascontiguousarray(words), np.ascontiguousarray(byte.astype(np.uint8).reshape(k // 512, 16, n))


def unpack_weight(words, scales, fmt):
    g, _, n = scales.shape
    words = np.ascontiguousarray(words).reshape(g, 128, n, -1)
    if fmt == "e4m3":
        vals = words.view(ml_dtypes.float8_e4m3fn).astype(np.float64)
    else:
        nib = np.empty((g, 128, n, 4), np.uint8)
        nib[..., 0::2] = words & 0xF
        nib[..., 1::2] = words >> 4
        vals = E2M1[nib]
    vals = vals * np.repeat(np.exp2(scales.astype(np.float64) - 127.0), 8, axis=1)[..., None]
    return vals.transpose(0, 1, 3, 2).reshape(g * 512, n)


D, T, U, I, Q = 512, 1024, 1024, 512, 128


def setup_inputs():
    n = np.random.standard_normal
    idx = np.stack([np.random.permutation(T)[:I] for _ in range(8)])
    idx2 = np.stack([np.random.permutation(U)[:I] for _ in range(8)])
    idx3 = np.stack([np.random.permutation(U)[:I] for _ in range(8)])
    fd = mx_kscale(D)
    keysp = pack_weight(n((D, T)) / fd[:, None], "e4m3")
    notesp = pack_weight(n((D, U)) / fd[:, None], "e2m1")
    return {
        "query": (n((D, Q)) * 1.0 / np.sqrt(D) * fd[:, None]).astype(np.float32),
        "keys_words": keysp[0],
        "keys_scales": keysp[1],
        "notes_words": notesp[0],
        "notes_scales": notesp[1],
        "offs": striped8(idx),
        "offs2": striped8(idx2),
        "offs3": striped8(idx3),
    }


def reference(query, keys_words, keys_scales, notes_words, notes_scales, offs, offs2, offs3):
    idx = unstriped8(offs)
    idx2 = unstriped8(offs2)
    idx3 = unstriped8(offs3)
    keysu = unpack_weight(keys_words, keys_scales, "e4m3")
    notesu = unpack_weight(notes_words, notes_scales, "e2m1")
    queryq = mxq(f64(query), 0, "e4m3")
    a = queryq.T @ keysu
    b = queryq.T @ notesu
    f1 = np.zeros((Q, U))
    f1[np.arange(Q)[:, None], idx2[np.arange(Q) % 128 // 16]] = pick8(a, idx, 16)
    cc = b + f1
    y = pick8(cc, idx3, 16) - pick8(b, idx2, 16)
    return y

@@ -1,0 +1,113 @@
+from contextlib import ExitStack
+
+import concourse.mybir as mybir
+
+D, T, U, I, Q = 512, 1024, 1024, 512, 128
+FLOPS = 2 * D * Q * (T + U)
+
+F32 = mybir.dt.float32
+BF16 = mybir.dt.bfloat16
+I32 = mybir.dt.int32
+U32 = mybir.dt.uint32
+U16 = mybir.dt.uint16
+U8 = mybir.dt.uint8
+FP8X4 = mybir.dt.float8_e4m3fn_x4
+FP4X4 = mybir.dt.float4_e2m1fn_x4
+COPY = mybir.ActivationFunctionType.Copy
+ADD = mybir.AluOpType.add
+SUB = mybir.AluOpType.subtract
+
+P = 128
+PACK = 4
+CHUNK = T // 4
+HALF = I // 2
+BANK = 512
+
+
+def tile_attend_crossed_two_kernel(tc, query, keys_words, keys_scales, notes_words, notes_scales,
+                                    offs, offs2, offs3, out):
+    nc = tc.nc
+    with ExitStack() as ctx:
+        sb = ctx.enter_context(tc.tile_pool(name="sb", bufs=1))
+        ps = ctx.enter_context(tc.psum_pool(name="ps", bufs=1))
+
+        idx = sb.tile([P, I // 16], U16, name="idx")
+        idx2 = sb.tile([P, I // 16], U16, name="idx2")
+        idx3 = sb.tile([P, I // 16], U16, name="idx3")
+        q_raw = sb.tile([P, PACK, Q], F32, name="q_raw", align_bytes=64)
+        q_bf = sb.tile([P, Q, PACK], BF16, name="q_bf", align_bytes=64)
+        q_codes = sb.tile([P, Q], U32, name="q_codes", align_bytes=64)
+        q_scales = sb.tile([P, Q], U8, name="q_scales", align_bytes=64)
+        k_codes = [sb.tile([P, T // 2], U32, name="k_codes%d" % h, align_bytes=64) for h in range(2)]
+        k_scales = sb.tile([P, CHUNK], U8, name="k_scales", align_bytes=64)
+        n_codes = sb.tile([P, 2 * U], U8, name="n_codes", align_bytes=64)
+        n_scales = sb.tile([P, U], U8, name="n_scales", align_bytes=64)
+        a = sb.tile([P, T], F32, name="a")
+        b = sb.tile([P, U], F32, name="b")
+        f1 = sb.tile([P, U], F32, name="f1")
+        cc = sb.tile([P, U], F32, name="cc")
+        a_picked = sb.tile([P, I], F32, name="a_picked")
+        b_picked = sb.tile([P, I], F32, name="b_picked")
+        cc_picked = sb.tile([P, HALF], F32, name="cc_picked")
+        res = [sb.tile([P, HALF], F32, name="res%d" % h) for h in range(2)]
+
+        nc.vector.memset(k_scales[:].bitcast(I32), 0)
+        nc.vector.memset(n_scales[:].bitcast(I32), 0)
+        nc.vector.memset(f1[:], 0.0)
+
+        nc.sync.dma_start(q_raw[:], query.rearrange("(p j) q -> p j q", j=PACK))
+        k_scale_words = keys_scales[0].bitcast(I32)
+        for quad in range(4):
+            nc.scalar.dma_start(
+                k_scales[32 * quad:32 * quad + 16, :].bitcast(I32),
+                k_scale_words[4 * quad:4 * quad + 4, :].rearrange("r (c n) -> c r n", c=4))
+        k_words = keys_words[0].rearrange("p t r -> p (t r)").bitcast(I32)
+        for h in range(2):
+            nc.sync.dma_start(k_codes[h][:].bitcast(I32), k_words[:, h * (T // 2):(h + 1) * (T // 2)])
+        nc.sync.dma_start(idx[:], offs)
+        nc.sync.dma_start(idx2[:], offs2)
+        nc.sync.dma_start(n_codes[:].bitcast(I32), notes_words[0].bitcast(I32))
+        n_scale_words = notes_scales[0].bitcast(I32)
+        for quad in range(4):
+            nc.sync.dma_start(n_scales[32 * quad:32 * quad + 4, :].bitcast(I32),
+                              n_scale_words[4 * quad:4 * quad + 4, :])
+        nc.sync.dma_start(idx3[:], offs3)
+
+        nc.vector.tensor_copy(q_bf[:], q_raw[:].rearrange("p j q -> p q j"))
+        nc.vector.quantize_mx(out=q_codes[:].bitcast(FP8X4), scales=q_scales[:],
+                              in_=q_bf[:].rearrange("p q j -> p (q j)"))
+
+        pieces = [(0, 256), (256, 256), (512, 256), (768, 128), (896, 128)]
+        for n, (first, width) in enumerate(pieces):
+            bank = ps.tile([P, width], F32, name="bank%d" % n)
+            c, in_chunk = divmod(first, CHUNK)
+            h, in_half = divmod(first, T // 2)
+            nc.tensor.matmul_mx(
+                out=bank[:], lhsT=q_codes[:].bitcast(FP8X4), lhsT_scale=q_scales[:],
+                rhs=k_codes[h][:, in_half:in_half + width].bitcast(FP8X4),
+                rhs_scale=k_scales[4 * c:, in_chunk:in_chunk + width], start=True, stop=True)
+            if n % 2 == 0:
+                nc.vector.tensor_copy(a[:, first:first + width], bank[:])
+            else:
+                nc.scalar.activation(a[:, first:first + width], bank[:], COPY)
+
+        nc.scalar.activation(a_picked[:, :HALF], a[:].indirect(idx[:, :HALF // 16]), COPY)
+        nc.vector.tensor_copy(a_picked[:, HALF:], a[:].indirect(idx[:, HALF // 16:]))
+        nc.vector.tensor_copy(f1[:].indirect(idx2[:]), a_picked[:])
+
+        for h in range(2):
+            bank = ps.tile([P, BANK], F32, name="bank%d" % (3 + h))
+            nc.tensor.matmul_mx(
+                out=bank[:], lhsT=q_codes[:].bitcast(FP8X4), lhsT_scale=q_scales[:],
+                rhs=n_codes[:, 2 * h * BANK:2 * (h + 1) * BANK].bitcast(FP4X4),
+                rhs_scale=n_scales[:, h * BANK:(h + 1) * BANK], start=True, stop=True)
+            nc.scalar.activation(b[:, h * BANK:(h + 1) * BANK], bank[:], COPY)
+        nc.scalar.activation(b_picked[:], b[:].indirect(idx2[:]), COPY)
+
+        nc.vector.tensor_tensor(cc[:], b[:], f1[:], ADD)
+
+        nc.vector.tensor_tensor(res[0][:], cc[:].indirect(idx3[:, :HALF // 16]), b_picked[:, :HALF], SUB)
+        nc.scalar.activation(cc_picked[:], cc[:].indirect(idx3[:, HALF // 16:]), COPY)
+        nc.vector.tensor_tensor(res[1][:], cc_picked[:], b_picked[:, HALF:], SUB)
+        for h in range(2):
+            nc.sync.dma_start(out[:, h * HALF:(h + 1) * HALF], res[h][:])

@@ -22,6 +22,7 @@ PACK = 4
 CHUNK = T // 4
 HALF = I // 2
 BANK = 512
+SPLIT = 704
 
 
 def tile_attend_crossed_two_kernel(tc, query, keys_words, keys_scales, notes_words, notes_scales,
@@ -58,7 +59,7 @@ def tile_attend_crossed_two_kernel(tc, query, keys_words, keys_scales, notes_wor
         nc.sync.dma_start(q_raw[:], query.rearrange("(p j) q -> p j q", j=PACK))
         k_scale_words = keys_scales[0].bitcast(I32)
         for quad in range(4):
-            nc.scalar.dma_start(
+            nc.sync.dma_start(
                 k_scales[32 * quad:32 * quad + 16, :].bitcast(I32),
                 k_scale_words[4 * quad:4 * quad + 4, :].rearrange("r (c n) -> c r n", c=4))
         k_words = keys_words[0].rearrange("p t r -> p (t r)").bitcast(I32)
@@ -73,7 +74,8 @@ def tile_attend_crossed_two_kernel(tc, query, keys_words, keys_scales, notes_wor
                               n_scale_words[4 * quad:4 * quad + 4, :])
         nc.sync.dma_start(idx3[:], offs3)
 
-        nc.vector.tensor_copy(q_bf[:], q_raw[:].rearrange("p j q -> p q j"))
+        nc.vector.tensor_copy(q_bf[:].rearrange("p (c i) j -> p c j i", i=4),
+                              q_raw[:].rearrange("p j (c i) -> p c j i", i=4))
         nc.vector.quantize_mx(out=q_codes[:].bitcast(FP8X4), scales=q_scales[:],
                               in_=q_bf[:].rearrange("p q j -> p (q j)"))
 
@@ -95,8 +97,10 @@ def tile_attend_crossed_two_kernel(tc, query, keys_words, keys_scales, notes_wor
         nc.vector.tensor_copy(a_picked[:, HALF:], a[:].indirect(idx[:, HALF // 16:]))
         nc.vector.tensor_copy(f1[:].indirect(idx2[:]), a_picked[:])
 
+        b_banks = []
         for h in range(2):
             bank = ps.tile([P, BANK], F32, name="bank%d" % (3 + h))
+            b_banks.append(bank)
             nc.tensor.matmul_mx(
                 out=bank[:], lhsT=q_codes[:].bitcast(FP8X4), lhsT_scale=q_scales[:],
                 rhs=n_codes[:, 2 * h * BANK:2 * (h + 1) * BANK].bitcast(FP4X4),
@@ -104,7 +108,9 @@ def tile_attend_crossed_two_kernel(tc, query, keys_words, keys_scales, notes_wor
             nc.scalar.activation(b[:, h * BANK:(h + 1) * BANK], bank[:], COPY)
         nc.scalar.activation(b_picked[:], b[:].indirect(idx2[:]), COPY)
 
-        nc.vector.tensor_tensor(cc[:], b[:], f1[:], ADD)
+        nc.gpsimd.tensor_tensor(cc[:, SPLIT:], f1[:, SPLIT:], b[:, SPLIT:], ADD)
+        nc.vector.tensor_tensor(cc[:, :BANK], f1[:, :BANK], b_banks[0][:], ADD)
+        nc.vector.tensor_tensor(cc[:, BANK:SPLIT], f1[:, BANK:SPLIT], b_banks[1][:, :SPLIT - BANK], ADD)
 
         nc.vector.tensor_tensor(res[0][:], cc[:].indirect(idx3[:, :HALF // 16]), b_picked[:, :HALF], SUB)
         nc.scalar.activation(cc_picked[:], cc[:].indirect(idx3[:, HALF // 16:]), COPY)

@@ -65,13 +65,13 @@ def tile_attend_crossed_two_kernel(tc, query, keys_words, keys_scales, notes_wor
         k_words = keys_words[0].rearrange("p t r -> p (t r)").bitcast(I32)
         for h in range(2):
             nc.sync.dma_start(k_codes[h][:].bitcast(I32), k_words[:, h * (T // 2):(h + 1) * (T // 2)])
-        nc.sync.dma_start(idx[:], offs)
-        nc.sync.dma_start(idx2[:], offs2)
         nc.sync.dma_start(n_codes[:].bitcast(I32), notes_words[0].bitcast(I32))
+        nc.sync.dma_start(idx[:], offs)
         n_scale_words = notes_scales[0].bitcast(I32)
         for quad in range(4):
             nc.sync.dma_start(n_scales[32 * quad:32 * quad + 4, :].bitcast(I32),
                               n_scale_words[4 * quad:4 * quad + 4, :])
+        nc.sync.dma_start(idx2[:], offs2)
         nc.sync.dma_start(idx3[:], offs3)
 
         nc.vector.tensor_copy(q_bf[:].rearrange("p (c i) j -> p c j i", i=4),

@@ -19,10 +19,15 @@ SUB = mybir.AluOpType.subtract
 
 P = 128
 PACK = 4
+QUADS = 4
+HEAD = 16
+BANK = 512
 CHUNK = T // 4
 HALF = I // 2
-BANK = 512
-SPLIT = 704
+HALF_COLS = HALF // HEAD
+VECTOR_ADDS = 704
+A_PIECES = [(0, CHUNK), (CHUNK, CHUNK), (2 * CHUNK, CHUNK),
+            (3 * CHUNK, CHUNK // 2), (3 * CHUNK + CHUNK // 2, CHUNK // 2)]
 
 
 def tile_attend_crossed_two_kernel(tc, query, keys_words, keys_scales, notes_words, notes_scales,
@@ -32,9 +37,9 @@ def tile_attend_crossed_two_kernel(tc, query, keys_words, keys_scales, notes_wor
         sb = ctx.enter_context(tc.tile_pool(name="sb", bufs=1))
         ps = ctx.enter_context(tc.psum_pool(name="ps", bufs=1))
 
-        idx = sb.tile([P, I // 16], U16, name="idx")
-        idx2 = sb.tile([P, I // 16], U16, name="idx2")
-        idx3 = sb.tile([P, I // 16], U16, name="idx3")
+        idx = sb.tile([P, I // HEAD], U16, name="idx")
+        idx2 = sb.tile([P, I // HEAD], U16, name="idx2")
+        idx3 = sb.tile([P, I // HEAD], U16, name="idx3")
         q_raw = sb.tile([P, PACK, Q], F32, name="q_raw", align_bytes=64)
         q_bf = sb.tile([P, Q, PACK], BF16, name="q_bf", align_bytes=64)
         q_codes = sb.tile([P, Q], U32, name="q_codes", align_bytes=64)
@@ -52,13 +57,11 @@ def tile_attend_crossed_two_kernel(tc, query, keys_words, keys_scales, notes_wor
         cc_picked = sb.tile([P, HALF], F32, name="cc_picked")
         res = [sb.tile([P, HALF], F32, name="res%d" % h) for h in range(2)]
 
-        nc.vector.memset(k_scales[:].bitcast(I32), 0)
-        nc.vector.memset(n_scales[:].bitcast(I32), 0)
         nc.vector.memset(f1[:], 0.0)
 
         nc.sync.dma_start(q_raw[:], query.rearrange("(p j) q -> p j q", j=PACK))
         k_scale_words = keys_scales[0].bitcast(I32)
-        for quad in range(4):
+        for quad in range(QUADS):
             nc.sync.dma_start(
                 k_scales[32 * quad:32 * quad + 16, :].bitcast(I32),
                 k_scale_words[4 * quad:4 * quad + 4, :].rearrange("r (c n) -> c r n", c=4))
@@ -68,7 +71,7 @@ def tile_attend_crossed_two_kernel(tc, query, keys_words, keys_scales, notes_wor
         nc.sync.dma_start(n_codes[:].bitcast(I32), notes_words[0].bitcast(I32))
         nc.sync.dma_start(idx[:], offs)
         n_scale_words = notes_scales[0].bitcast(I32)
-        for quad in range(4):
+        for quad in range(QUADS):
             nc.sync.dma_start(n_scales[32 * quad:32 * quad + 4, :].bitcast(I32),
                               n_scale_words[4 * quad:4 * quad + 4, :])
         nc.sync.dma_start(idx2[:], offs2)
@@ -79,8 +82,7 @@ def tile_attend_crossed_two_kernel(tc, query, keys_words, keys_scales, notes_wor
         nc.vector.quantize_mx(out=q_codes[:].bitcast(FP8X4), scales=q_scales[:],
                               in_=q_bf[:].rearrange("p q j -> p (q j)"))
 
-        pieces = [(0, 256), (256, 256), (512, 256), (768, 128), (896, 128)]
-        for n, (first, width) in enumerate(pieces):
+        for n, (first, width) in enumerate(A_PIECES):
             bank = ps.tile([P, width], F32, name="bank%d" % n)
             c, in_chunk = divmod(first, CHUNK)
             h, in_half = divmod(first, T // 2)
@@ -93,13 +95,13 @@ def tile_attend_crossed_two_kernel(tc, query, keys_words, keys_scales, notes_wor
             else:
                 nc.scalar.activation(a[:, first:first + width], bank[:], COPY)
 
-        nc.scalar.activation(a_picked[:, :HALF], a[:].indirect(idx[:, :HALF // 16]), COPY)
-        nc.vector.tensor_copy(a_picked[:, HALF:], a[:].indirect(idx[:, HALF // 16:]))
+        nc.scalar.activation(a_picked[:, :HALF], a[:].indirect(idx[:, :HALF_COLS]), COPY)
+        nc.vector.tensor_copy(a_picked[:, HALF:], a[:].indirect(idx[:, HALF_COLS:]))
         nc.vector.tensor_copy(f1[:].indirect(idx2[:]), a_picked[:])
 
         b_banks = []
         for h in range(2):
-            bank = ps.tile([P, BANK], F32, name="bank%d" % (3 + h))
+            bank = ps.tile([P, BANK], F32, name="bank%d" % (len(A_PIECES) - 2 + h))
             b_banks.append(bank)
             nc.tensor.matmul_mx(
                 out=bank[:], lhsT=q_codes[:].bitcast(FP8X4), lhsT_scale=q_scales[:],
@@ -108,12 +110,13 @@ def tile_attend_crossed_two_kernel(tc, query, keys_words, keys_scales, notes_wor
             nc.scalar.activation(b[:, h * BANK:(h + 1) * BANK], bank[:], COPY)
         nc.scalar.activation(b_picked[:], b[:].indirect(idx2[:]), COPY)
 
-        nc.gpsimd.tensor_tensor(cc[:, SPLIT:], f1[:, SPLIT:], b[:, SPLIT:], ADD)
+        nc.gpsimd.tensor_tensor(cc[:, VECTOR_ADDS:], f1[:, VECTOR_ADDS:], b[:, VECTOR_ADDS:], ADD)
         nc.vector.tensor_tensor(cc[:, :BANK], f1[:, :BANK], b_banks[0][:], ADD)
-        nc.vector.tensor_tensor(cc[:, BANK:SPLIT], f1[:, BANK:SPLIT], b_banks[1][:, :SPLIT - BANK], ADD)
+        nc.vector.tensor_tensor(cc[:, BANK:VECTOR_ADDS], f1[:, BANK:VECTOR_ADDS],
+                                b_banks[1][:, :VECTOR_ADDS - BANK], ADD)
 
-        nc.vector.tensor_tensor(res[0][:], cc[:].indirect(idx3[:, :HALF // 16]), b_picked[:, :HALF], SUB)
-        nc.scalar.activation(cc_picked[:], cc[:].indirect(idx3[:, HALF // 16:]), COPY)
+        nc.vector.tensor_tensor(res[0][:], cc[:].indirect(idx3[:, :HALF_COLS]), b_picked[:, :HALF], SUB)
+        nc.scalar.activation(cc_picked[:], cc[:].indirect(idx3[:, HALF_COLS:]), COPY)
         nc.vector.tensor_tensor(res[1][:], cc_picked[:], b_picked[:, HALF:], SUB)
         for h in range(2):
             nc.sync.dma_start(out[:, h * HALF:(h + 1) * HALF], res[h][:])

from contextlib import ExitStack

import concourse.mybir as mybir

D, T, U, I, Q = 512, 1024, 1024, 512, 128
FLOPS = 2 * D * Q * (T + U)

F32 = mybir.dt.float32
BF16 = mybir.dt.bfloat16
I32 = mybir.dt.int32
U32 = mybir.dt.uint32
U16 = mybir.dt.uint16
U8 = mybir.dt.uint8
FP8X4 = mybir.dt.float8_e4m3fn_x4
FP4X4 = mybir.dt.float4_e2m1fn_x4
COPY = mybir.ActivationFunctionType.Copy
ADD = mybir.AluOpType.add
SUB = mybir.AluOpType.subtract

P = 128
PACK = 4
QUADS = 4
HEAD = 16
BANK = 512
CHUNK = T // 4
HALF = I // 2
HALF_COLS = HALF // HEAD
VECTOR_ADDS = 704
A_PIECES = [(0, CHUNK), (CHUNK, CHUNK), (2 * CHUNK, CHUNK),
            (3 * CHUNK, CHUNK // 2), (3 * CHUNK + CHUNK // 2, CHUNK // 2)]


def tile_attend_crossed_two_kernel(tc, query, keys_words, keys_scales, notes_words, notes_scales,
                                    offs, offs2, offs3, out):
    nc = tc.nc
    with ExitStack() as ctx:
        sb = ctx.enter_context(tc.tile_pool(name="sb", bufs=1))
        ps = ctx.enter_context(tc.psum_pool(name="ps", bufs=1))

        idx = sb.tile([P, I // HEAD], U16, name="idx")
        idx2 = sb.tile([P, I // HEAD], U16, name="idx2")
        idx3 = sb.tile([P, I // HEAD], U16, name="idx3")
        q_raw = sb.tile([P, PACK, Q], F32, name="q_raw", align_bytes=64)
        q_bf = sb.tile([P, Q, PACK], BF16, name="q_bf", align_bytes=64)
        q_codes = sb.tile([P, Q], U32, name="q_codes", align_bytes=64)
        q_scales = sb.tile([P, Q], U8, name="q_scales", align_bytes=64)
        k_codes = [sb.tile([P, T // 2], U32, name="k_codes%d" % h, align_bytes=64) for h in range(2)]
        k_scales = sb.tile([P, CHUNK], U8, name="k_scales", align_bytes=64)
        n_codes = sb.tile([P, 2 * U], U8, name="n_codes", align_bytes=64)
        n_scales = sb.tile([P, U], U8, name="n_scales", align_bytes=64)
        a = sb.tile([P, T], F32, name="a")
        b = sb.tile([P, U], F32, name="b")
        f1 = sb.tile([P, U], F32, name="f1")
        cc = sb.tile([P, U], F32, name="cc")
        a_picked = sb.tile([P, I], F32, name="a_picked")
        b_picked = sb.tile([P, I], F32, name="b_picked")
        cc_picked = sb.tile([P, HALF], F32, name="cc_picked")
        res = [sb.tile([P, HALF], F32, name="res%d" % h) for h in range(2)]

        nc.vector.memset(f1[:], 0.0)

        nc.sync.dma_start(q_raw[:], query.rearrange("(p j) q -> p j q", j=PACK))
        k_scale_words = keys_scales[0].bitcast(I32)
        for quad in range(QUADS):
            nc.sync.dma_start(
                k_scales[32 * quad:32 * quad + 16, :].bitcast(I32),
                k_scale_words[4 * quad:4 * quad + 4, :].rearrange("r (c n) -> c r n", c=4))
        k_words = keys_words[0].rearrange("p t r -> p (t r)").bitcast(I32)
        for h in range(2):
            nc.sync.dma_start(k_codes[h][:].bitcast(I32), k_words[:, h * (T // 2):(h + 1) * (T // 2)])
        nc.sync.dma_start(n_codes[:].bitcast(I32), notes_words[0].bitcast(I32))
        nc.sync.dma_start(idx[:], offs)
        n_scale_words = notes_scales[0].bitcast(I32)
        for quad in range(QUADS):
            nc.sync.dma_start(n_scales[32 * quad:32 * quad + 4, :].bitcast(I32),
                              n_scale_words[4 * quad:4 * quad + 4, :])
        nc.sync.dma_start(idx2[:], offs2)
        nc.sync.dma_start(idx3[:], offs3)

        nc.vector.tensor_copy(q_bf[:].rearrange("p (c i) j -> p c j i", i=4),
                              q_raw[:].rearrange("p j (c i) -> p c j i", i=4))
        nc.vector.quantize_mx(out=q_codes[:].bitcast(FP8X4), scales=q_scales[:],
                              in_=q_bf[:].rearrange("p q j -> p (q j)"))

        for n, (first, width) in enumerate(A_PIECES):
            bank = ps.tile([P, width], F32, name="bank%d" % n)
            c, in_chunk = divmod(first, CHUNK)
            h, in_half = divmod(first, T // 2)
            nc.tensor.matmul_mx(
                out=bank[:], lhsT=q_codes[:].bitcast(FP8X4), lhsT_scale=q_scales[:],
                rhs=k_codes[h][:, in_half:in_half + width].bitcast(FP8X4),
                rhs_scale=k_scales[4 * c:, in_chunk:in_chunk + width], start=True, stop=True)
            if n % 2 == 0:
                nc.vector.tensor_copy(a[:, first:first + width], bank[:])
            else:
                nc.scalar.activation(a[:, first:first + width], bank[:], COPY)

        nc.scalar.activation(a_picked[:, :HALF], a[:].indirect(idx[:, :HALF_COLS]), COPY)
        nc.vector.tensor_copy(a_picked[:, HALF:], a[:].indirect(idx[:, HALF_COLS:]))
        nc.vector.tensor_copy(f1[:].indirect(idx2[:]), a_picked[:])

        b_banks = []
        for h in range(2):
            bank = ps.tile([P, BANK], F32, name="bank%d" % (len(A_PIECES) - 2 + h))
            b_banks.append(bank)
            nc.tensor.matmul_mx(
                out=bank[:], lhsT=q_codes[:].bitcast(FP8X4), lhsT_scale=q_scales[:],
                rhs=n_codes[:, 2 * h * BANK:2 * (h + 1) * BANK].bitcast(FP4X4),
                rhs_scale=n_scales[:, h * BANK:(h + 1) * BANK], start=True, stop=True)
            nc.scalar.activation(b[:, h * BANK:(h + 1) * BANK], bank[:], COPY)
        nc.scalar.activation(b_picked[:], b[:].indirect(idx2[:]), COPY)

        nc.gpsimd.tensor_tensor(cc[:, VECTOR_ADDS:], f1[:, VECTOR_ADDS:], b[:, VECTOR_ADDS:], ADD)
        nc.vector.tensor_tensor(cc[:, :BANK], f1[:, :BANK], b_banks[0][:], ADD)
        nc.vector.tensor_tensor(cc[:, BANK:VECTOR_ADDS], f1[:, BANK:VECTOR_ADDS],
                                b_banks[1][:, :VECTOR_ADDS - BANK], ADD)

        nc.vector.tensor_tensor(res[0][:], cc[:].indirect(idx3[:, :HALF_COLS]), b_picked[:, :HALF], SUB)
        nc.scalar.activation(cc_picked[:], cc[:].indirect(idx3[:, HALF_COLS:]), COPY)
        nc.vector.tensor_tensor(res[1][:], cc_picked[:], b_picked[:, HALF:], SUB)
        for h in range(2):
            nc.sync.dma_start(out[:, h * HALF:(h + 1) * HALF], res[h][:])
